import numpy as np
import ml_dtypes


def mxq(x, axis, fmt="e4m3"):
    dtype, down = {"e4m3": (ml_dtypes.float8_e4m3fn, 7), "e5m2": (ml_dtypes.float8_e5m2, 14)}[fmt]
    v = np.moveaxis(np.asarray(x, np.float32).astype(ml_dtypes.bfloat16).astype(np.float64), axis, -1)
    blocks = v.reshape(v.shape[:-1] + (-1, 32))
    amax = np.abs(blocks).max(-1, keepdims=True)
    byte = np.maximum(np.where(amax > 0, np.frexp(amax)[1] - 1 + 127, 0) - down, 1)
    scale = np.exp2(byte - 127.0)
    codes = (blocks / scale).astype(np.float32).astype(dtype).astype(np.float64)
    return np.moveaxis((codes * scale).reshape(v.shape), -1, axis)


WIDE = False


def mx_kscale(k):
    if not WIDE:
        return np.ones(k)
    levels = np.array([10, -10, 5, -5, 0])
    if k % 512:
        return np.exp2(np.random.permutation(np.resize(levels, k // 32))).repeat(32)
    a = np.empty((k // 512, 16))
    for p in range(k // 512):
        a[p, :8] = np.random.permutation(np.resize(levels, 8))
        for g in range(8):
            far = levels[np.abs(levels - a[p, g]) >= 10]
            a[p, g + 8] = far[np.random.randint(len(far))]
    return np.exp2(a.ravel()).repeat(32)


def f64(x):
    return np.asarray(x).astype(np.float64)


def planes(y):
    n, m = y.shape
    v = y.astype(np.float32).astype(ml_dtypes.bfloat16).astype(np.float64).reshape(n // 32, 32, m)
    top = np.abs(v).max(1)
    byte = np.clip(np.where(top > 0, np.frexp(top)[1] - 1 + 127 - 7, 1), 1, 254)
    codes = (v * np.exp2(127.0 - byte)[:, None, :]).reshape(n, m).astype(np.float32).astype(ml_dtypes.float8_e4m3fn).view(np.uint8)
    words = codes.reshape(n // 512, 128, 4, m).transpose(0, 1, 3, 2)
    return np.ascontiguousarray(words), np.ascontiguousarray(byte.astype(np.uint8).reshape(n // 512, 16, m))


def split(x):
    m, e = np.frexp(f64(x))
    hi = np.ldexp(np.trunc(16.0 * m) / 16.0, e)
    return hi, f64(x) - hi


K, M, T = 512, 512, 1024


def setup_inputs():
    n = np.random.standard_normal
    s = mx_kscale(K)[:, None]
    return {
        "w": (n((K, M)) / np.sqrt(K) / s).astype(np.float32),
        "x": (n((K, T)) * s).astype(np.float32),
    }


def reference(w, x):
    w_hi, w_lo = split(w)
    w_hi_, w_lo_ = mxq(w_hi, 0, "e4m3"), mxq(w_lo, 0, "e4m3")
    x_hi, x_lo = split(x)
    x_hi_, x_lo_ = mxq(x_hi, 0, "e4m3"), mxq(x_lo, 0, "e4m3")
    y = x_hi_.T @ w_hi_ + x_lo_.T @ w_hi_ + x_hi_.T @ w_lo_
    out_0 = np.maximum(y, 0.0) ** 2
    return (out_0,) + planes(out_0)

@@ -1,0 +1,271 @@
+from contextlib import ExitStack
+
+import concourse.mybir as mybir
+
+K, M, T = 512, 512, 1024
+FLOPS = 3 * 2 * K * M * T
+
+F32 = mybir.dt.float32
+BF16 = mybir.dt.bfloat16
+I32 = mybir.dt.int32
+U8 = mybir.dt.uint8
+FP8X4 = mybir.dt.float8_e4m3fn_x4
+ACT = mybir.ActivationFunctionType
+ALU = mybir.AluOpType
+
+P = 128
+PACK = 4
+HALF_N = 256
+KEEP_HI = -983056
+
+
+def tile_mix_split3_tm_pl_relu2_kernel(tc, w, x, out_0, out_1, out_2):
+    nc = tc.nc
+    with ExitStack() as ctx:
+        sb = ctx.enter_context(tc.tile_pool(name="sb", bufs=1))
+        ps = ctx.enter_context(tc.psum_pool(name="ps", bufs=1))
+        ctx.enter_context(tc.manual_schedule())
+
+        w_rows = w.rearrange("(p j) n -> p j n", j=PACK)
+        x_rows = x.rearrange("(p j) t -> p j t", j=PACK)
+        out_rows = out_0.rearrange("(a p r) n -> a p r n", a=2, r=PACK)
+
+        raw = {}
+        parts = {}
+        codes = {}
+        scales = {}
+        for key in ("w0", "w1", "x00", "x01", "x10", "x11"):
+            for part in ("hi", "lo"):
+                parts[key, part] = sb.tile([P, 1024], BF16, name="b_%s_%s" % (key, part), align_bytes=64)
+                codes[key, part] = sb.tile([P, 256], I32, name="c_%s_%s" % (key, part), align_bytes=64)
+                scales[key, part] = sb.tile([P, 256], U8, name="s_%s_%s" % (key, part), align_bytes=64)
+
+        def load(name, rows, c0, c1):
+            raw[name] = sb.tile([P, PACK, c1 - c0], F32, name="raw_" + name, align_bytes=64)
+            nc.sync.dma_start(out=raw[name][:], in_=rows[:, :, c0:c1])
+
+        def w_piece(name, key, n0, n1):
+            src = raw[name][:].rearrange("p j (c i) -> p c j i", i=2)
+            top = raw[name][:].bitcast(BF16).rearrange("p j (c i h) -> p c j i h", i=2, h=2)[:, :, :, :, 1]
+            hi = parts[key, "hi"][:, PACK * n0 : PACK * n1]
+            lo = parts[key, "lo"][:, PACK * n0 : PACK * n1]
+            return (
+                src,
+                top,
+                hi.rearrange("p (c i j) -> p c j i", i=2, j=PACK),
+                lo.rearrange("p (c i j) -> p c j i", i=2, j=PACK),
+                hi.bitcast(I32),
+            )
+
+        def x_piece(name, key, rp, m0, m1):
+            rs = slice(2 * rp, 2 * rp + 2)
+            src = raw[name][:].rearrange("p j (m r) -> p m j r", r=PACK)[:, :, :, rs]
+            top = raw[name][:].bitcast(BF16).rearrange("p j (m r h) -> p m j r h", r=PACK, h=2)[:, :, :, rs, 1]
+            hi = parts[key, "hi"][:].rearrange("p (r e) -> p r e", r=2)[:, :, PACK * m0 : PACK * m1]
+            lo = parts[key, "lo"][:].rearrange("p (r e) -> p r e", r=2)[:, :, PACK * m0 : PACK * m1]
+            return (
+                src,
+                top,
+                hi.rearrange("p r (m j) -> p m j r", j=PACK),
+                lo.rearrange("p r (m j) -> p m j r", j=PACK),
+                hi.bitcast(I32),
+            )
+
+        def top(piece):
+            nc.scalar.copy(out=piece[2], in_=piece[1])
+
+        def mask(piece):
+            nc.vector.tensor_scalar(out=piece[4], in0=piece[4], scalar1=KEEP_HI, scalar2=None, op0=ALU.bitwise_and)
+
+        def rest(piece):
+            nc.vector.tensor_tensor(out=piece[3], in0=piece[0], in1=piece[2], op=ALU.subtract)
+
+        def quant(key, part, c0=0, c1=256):
+            nc.vector.quantize_mx(
+                out=codes[key, part][:, c0:c1].bitcast(FP8X4),
+                scales=scales[key, part][:, c0:c1],
+                in_=parts[key, part][:, PACK * c0 : PACK * c1],
+            )
+
+        acc = {}
+        relu = {}
+        res = {}
+        res16 = {}
+        out_codes = {}
+        out_scales = {}
+        for a in range(2):
+            out_scales[a] = sb.tile([P, M], U8, name="os_%d" % a, align_bytes=64)
+            for h in range(2):
+                res[a, h] = sb.tile([P, PACK, HALF_N], F32, name="res_%d_%d" % (a, h), align_bytes=64)
+                res16[a, h] = sb.tile([P, PACK * HALF_N], BF16, name="res16_%d_%d" % (a, h), align_bytes=64)
+                out_codes[a, h] = sb.tile([P, HALF_N], I32, name="oc_%d_%d" % (a, h), align_bytes=64)
+                for rp in range(2):
+                    acc[a, rp, h] = ps.tile([P, 2, HALF_N], F32, name="acc_%d_%d_%d" % (a, rp, h))
+                    relu[a, rp, h] = sb.tile([P, 2, HALF_N], F32, name="relu_%d_%d_%d" % (a, rp, h), align_bytes=64)
+
+        def mm(a, rp, h):
+            xk = "x%d%d" % (a, rp)
+            wk = "w%d" % h
+            for r in range(2):
+                cols = slice(r * P, (r + 1) * P)
+                for i, (xp, wp) in enumerate((("hi", "hi"), ("hi", "lo"), ("lo", "hi"))):
+                    nc.tensor.matmul_mx(
+                        out=acc[a, rp, h][:, r, :],
+                        lhsT=codes[xk, xp][:, cols].bitcast(FP8X4),
+                        lhsT_scale=scales[xk, xp][:, cols],
+                        rhs=codes[wk, wp][:].bitcast(FP8X4),
+                        rhs_scale=scales[wk, wp][:],
+                        start=(i == 0),
+                        stop=(i == 2),
+                    )
+
+        def relu_s(a, rp, h):
+            nc.scalar.activation(out=relu[a, rp, h][:], in_=acc[a, rp, h][:], func=ACT.Relu)
+
+        def relu_v(a, rp, h):
+            nc.vector.tensor_scalar(out=relu[a, rp, h][:], in0=acc[a, rp, h][:], scalar1=0.0, scalar2=None, op0=ALU.max)
+
+        def square(a, rp, h):
+            nc.scalar.activation(out=res[a, h][:, 2 * rp : 2 * rp + 2, :], in_=relu[a, rp, h][:], func=ACT.Square)
+
+        def store_res(a, rp, h, eng=nc.sync):
+            eng.dma_start(
+                out=out_rows[a][:, 2 * rp : 2 * rp + 2, h * HALF_N : (h + 1) * HALF_N],
+                in_=res[a, h][:, 2 * rp : 2 * rp + 2, :],
+            )
+
+        def cast(a, h):
+            nc.vector.tensor_copy(
+                out=res16[a, h][:].rearrange("p (c i r) -> p c r i", i=2, r=PACK),
+                in_=res[a, h][:].rearrange("p r (c i) -> p c r i", i=2),
+            )
+
+        def quant_out(a, h):
+            nc.vector.quantize_mx(
+                out=out_codes[a, h][:].bitcast(FP8X4),
+                scales=out_scales[a][:, h * HALF_N : (h + 1) * HALF_N],
+                in_=res16[a, h][:],
+            )
+
+        def store_codes(a, h, eng=nc.sync):
+            words = out_1[a].rearrange("p n i -> p (n i)").bitcast(I32)
+            eng.dma_start(out=words[:, h * HALF_N : (h + 1) * HALF_N], in_=out_codes[a, h][:])
+
+        def store_scales(a, q, eng=nc.sync):
+            eng.dma_start(
+                out=out_2[a, 4 * q : 4 * q + 4, :].bitcast(I32),
+                in_=out_scales[a][32 * q : 32 * q + 4, :].bitcast(I32),
+            )
+
+        load("wa", w_rows, 0, 128)
+        load("wb", w_rows, 128, 256)
+        load("xa", x_rows, 0, 256)
+        load("xb", x_rows, 256, 512)
+        load("wc", w_rows, 256, 512)
+        load("xc", x_rows, 512, 1024)
+
+        warm = sb.tile([P, 1], F32, name="warm")
+        nc.gpsimd.memset(warm[:], 0.0)
+        warm_out = sb.tile([P, 1], F32, name="warm_out")
+        nc.scalar.activation(out=warm_out[:], in_=warm[:], func=ACT.Square)
+
+        wa = w_piece("wa", "w0", 0, 128)
+        wb = w_piece("wb", "w0", 128, 256)
+        wc = w_piece("wc", "w1", 0, 256)
+        xa0 = x_piece("xa", "x00", 0, 0, 64)
+        xa1 = x_piece("xa", "x01", 1, 0, 64)
+        xb0 = x_piece("xb", "x00", 0, 64, 128)
+        xb1 = x_piece("xb", "x01", 1, 64, 128)
+        xc0 = x_piece("xc", "x10", 0, 0, 128)
+        xc1 = x_piece("xc", "x11", 1, 0, 128)
+
+        top(wa)
+        mask(wa)
+        rest(wa)
+        top(wb)
+        mask(wb)
+        quant("w0", "lo", 0, 128)
+        rest(wb)
+        quant("w0", "hi")
+        top(xa0)
+        top(xa1)
+        mask(xa0)
+        quant("w0", "lo", 128, 256)
+        rest(xa0)
+        mask(xa1)
+        top(xb0)
+        top(xb1)
+        mask(xb0)
+        rest(xa1)
+        rest(xb0)
+        quant("x00", "hi")
+        mask(xb1)
+        quant("x00", "lo")
+        mm(0, 0, 0)
+        rest(xb1)
+        quant("x01", "hi")
+        top(wc)
+        mask(wc)
+        quant("x01", "lo")
+        mm(0, 1, 0)
+        relu_s(0, 0, 0)
+        top(xc0)
+        square(0, 0, 0)
+        store_res(0, 0, 0)
+        rest(wc)
+        quant("w1", "hi")
+        mask(xc0)
+        quant("w1", "lo")
+        mm(0, 0, 1)
+        mm(0, 1, 1)
+        relu_s(0, 1, 0)
+        top(xc1)
+        square(0, 1, 0)
+        store_res(0, 1, 0)
+        rest(xc0)
+        quant("x10", "hi")
+        mask(xc1)
+        quant("x10", "lo")
+        mm(1, 0, 0)
+        mm(1, 0, 1)
+        relu_s(0, 0, 1)
+        relu_s(0, 1, 1)
+        square(0, 0, 1)
+        store_res(0, 0, 1)
+        square(0, 1, 1)
+        store_res(0, 1, 1)
+        rest(xc1)
+        quant("x11", "hi")
+        cast(0, 0)
+        quant("x11", "lo")
+        mm(1, 1, 0)
+        mm(1, 1, 1)
+        quant_out(0, 0)
+        store_codes(0, 0)
+        relu_s(1, 0, 0)
+        relu_s(1, 0, 1)
+        square(1, 0, 0)
+        store_res(1, 0, 0)
+        cast(0, 1)
+        relu_v(1, 1, 0)
+        quant_out(0, 1)
+        store_codes(0, 1)
+        for q in range(4):
+            store_scales(0, q)
+        square(1, 1, 0)
+        store_res(1, 1, 0)
+        relu_s(1, 1, 1)
+        square(1, 0, 1)
+        store_res(1, 0, 1)
+        square(1, 1, 1)
+        store_res(1, 1, 1)
+        cast(1, 0)
+        cast(1, 1)
+        quant_out(1, 0)
+        store_codes(1, 0)
+        quant_out(1, 1)
+        store_codes(1, 1)
+        store_scales(1, 0, nc.scalar)
+        store_scales(1, 1)
+        store_scales(1, 2, nc.scalar)
+        store_scales(1, 3)

@@ -71,8 +71,11 @@ def tile_mix_split3_tm_pl_relu2_kernel(tc, w, x, out_0, out_1, out_2):
                 hi.bitcast(I32),
             )
 
-        def top(piece):
+        def top_s(piece):
             nc.scalar.copy(out=piece[2], in_=piece[1])
+
+        def top_v(piece):
+            nc.vector.tensor_copy(out=piece[2], in_=piece[1])
 
         def mask(piece):
             nc.vector.tensor_scalar(out=piece[4], in0=piece[4], scalar1=KEEP_HI, scalar2=None, op0=ALU.bitwise_and)
@@ -92,9 +95,8 @@ def tile_mix_split3_tm_pl_relu2_kernel(tc, w, x, out_0, out_1, out_2):
         res = {}
         res16 = {}
         out_codes = {}
-        out_scales = {}
+        out_scales = sb.tile([P, 2, M], U8, name="out_scales", align_bytes=64)
         for a in range(2):
-            out_scales[a] = sb.tile([P, M], U8, name="os_%d" % a, align_bytes=64)
             for h in range(2):
                 res[a, h] = sb.tile([P, PACK, HALF_N], F32, name="res_%d_%d" % (a, h), align_bytes=64)
                 res16[a, h] = sb.tile([P, PACK * HALF_N], BF16, name="res16_%d_%d" % (a, h), align_bytes=64)
@@ -103,21 +105,20 @@ def tile_mix_split3_tm_pl_relu2_kernel(tc, w, x, out_0, out_1, out_2):
                     acc[a, rp, h] = ps.tile([P, 2, HALF_N], F32, name="acc_%d_%d_%d" % (a, rp, h))
                     relu[a, rp, h] = sb.tile([P, 2, HALF_N], F32, name="relu_%d_%d_%d" % (a, rp, h), align_bytes=64)
 
-        def mm(a, rp, h):
+        def mm(a, rp, h, r):
             xk = "x%d%d" % (a, rp)
             wk = "w%d" % h
-            for r in range(2):
-                cols = slice(r * P, (r + 1) * P)
-                for i, (xp, wp) in enumerate((("hi", "hi"), ("hi", "lo"), ("lo", "hi"))):
-                    nc.tensor.matmul_mx(
-                        out=acc[a, rp, h][:, r, :],
-                        lhsT=codes[xk, xp][:, cols].bitcast(FP8X4),
-                        lhsT_scale=scales[xk, xp][:, cols],
-                        rhs=codes[wk, wp][:].bitcast(FP8X4),
-                        rhs_scale=scales[wk, wp][:],
-                        start=(i == 0),
-                        stop=(i == 2),
-                    )
+            cols = slice(r * P, (r + 1) * P)
+            for i, (xp, wp) in enumerate((("hi", "hi"), ("hi", "lo"), ("lo", "hi"))):
+                nc.tensor.matmul_mx(
+                    out=acc[a, rp, h][:, r, :],
+                    lhsT=codes[xk, xp][:, cols].bitcast(FP8X4),
+                    lhsT_scale=scales[xk, xp][:, cols],
+                    rhs=codes[wk, wp][:].bitcast(FP8X4),
+                    rhs_scale=scales[wk, wp][:],
+                    start=(i == 0),
+                    stop=(i == 2),
+                )
 
         def relu_s(a, rp, h):
             nc.scalar.activation(out=relu[a, rp, h][:], in_=acc[a, rp, h][:], func=ACT.Relu)
@@ -125,8 +126,13 @@ def tile_mix_split3_tm_pl_relu2_kernel(tc, w, x, out_0, out_1, out_2):
         def relu_v(a, rp, h):
             nc.vector.tensor_scalar(out=relu[a, rp, h][:], in0=acc[a, rp, h][:], scalar1=0.0, scalar2=None, op0=ALU.max)
 
-        def square(a, rp, h):
+        def square_s(a, rp, h):
             nc.scalar.activation(out=res[a, h][:, 2 * rp : 2 * rp + 2, :], in_=relu[a, rp, h][:], func=ACT.Square)
+
+        def square_v(a, rp, h):
+            nc.vector.tensor_tensor(
+                out=res[a, h][:, 2 * rp : 2 * rp + 2, :], in0=relu[a, rp, h][:], in1=relu[a, rp, h][:], op=ALU.mult
+            )
 
         def store_res(a, rp, h, eng=nc.sync):
             eng.dma_start(
@@ -134,27 +140,34 @@ def tile_mix_split3_tm_pl_relu2_kernel(tc, w, x, out_0, out_1, out_2):
                 in_=res[a, h][:, 2 * rp : 2 * rp + 2, :],
             )
 
-        def cast(a, h):
-            nc.vector.tensor_copy(
-                out=res16[a, h][:].rearrange("p (c i r) -> p c r i", i=2, r=PACK),
-                in_=res[a, h][:].rearrange("p r (c i) -> p c r i", i=2),
-            )
+        def cast_views(a, h, c0, c1):
+            dst = res16[a, h][:, PACK * c0 : PACK * c1].rearrange("p (c i r) -> p c r i", i=2, r=PACK)
+            src = res[a, h][:, :, c0:c1].rearrange("p r (c i) -> p c r i", i=2)
+            return dst, src
 
-        def quant_out(a, h):
+        def cast_v(a, h, c0, c1):
+            dst, src = cast_views(a, h, c0, c1)
+            nc.vector.tensor_copy(out=dst, in_=src)
+
+        def cast_s(a, h, c0, c1):
+            dst, src = cast_views(a, h, c0, c1)
+            nc.scalar.copy(out=dst, in_=src)
+
+        def quant_out(a, h, c0, c1):
             nc.vector.quantize_mx(
-                out=out_codes[a, h][:].bitcast(FP8X4),
-                scales=out_scales[a][:, h * HALF_N : (h + 1) * HALF_N],
-                in_=res16[a, h][:],
+                out=out_codes[a, h][:, c0:c1].bitcast(FP8X4),
+                scales=out_scales[:, a, h * HALF_N + c0 : h * HALF_N + c1],
+                in_=res16[a, h][:, PACK * c0 : PACK * c1],
             )
 
         def store_codes(a, h, eng=nc.sync):
             words = out_1[a].rearrange("p n i -> p (n i)").bitcast(I32)
             eng.dma_start(out=words[:, h * HALF_N : (h + 1) * HALF_N], in_=out_codes[a, h][:])
 
-        def store_scales(a, q, eng=nc.sync):
+        def store_scales(q, eng=nc.sync):
             eng.dma_start(
-                out=out_2[a, 4 * q : 4 * q + 4, :].bitcast(I32),
-                in_=out_scales[a][32 * q : 32 * q + 4, :].bitcast(I32),
+                out=out_2[:, 4 * q : 4 * q + 4, :].rearrange("a q n -> q a n").bitcast(I32),
+                in_=out_scales[32 * q : 32 * q + 4, :, :].bitcast(I32),
             )
 
         load("wa", w_rows, 0, 128)
@@ -162,7 +175,8 @@ def tile_mix_split3_tm_pl_relu2_kernel(tc, w, x, out_0, out_1, out_2):
         load("xa", x_rows, 0, 256)
         load("xb", x_rows, 256, 512)
         load("wc", w_rows, 256, 512)
-        load("xc", x_rows, 512, 1024)
+        load("xc", x_rows, 512, 768)
+        load("xd", x_rows, 768, 1024)
 
         warm = sb.tile([P, 1], F32, name="warm")
         nc.gpsimd.memset(warm[:], 0.0)
@@ -176,96 +190,111 @@ def tile_mix_split3_tm_pl_relu2_kernel(tc, w, x, out_0, out_1, out_2):
         xa1 = x_piece("xa", "x01", 1, 0, 64)
         xb0 = x_piece("xb", "x00", 0, 64, 128)
         xb1 = x_piece("xb", "x01", 1, 64, 128)
-        xc0 = x_piece("xc", "x10", 0, 0, 128)
-        xc1 = x_piece("xc", "x11", 1, 0, 128)
+        xc0 = x_piece("xc", "x10", 0, 0, 64)
+        xc1 = x_piece("xc", "x11", 1, 0, 64)
+        xd0 = x_piece("xd", "x10", 0, 64, 128)
+        xd1 = x_piece("xd", "x11", 1, 64, 128)
 
-        top(wa)
+        top_v(wa)
+        top_s(wb)
         mask(wa)
         rest(wa)
-        top(wb)
         mask(wb)
-        quant("w0", "lo", 0, 128)
+        top_s(xa0)
+        top_s(xa1)
         rest(wb)
-        quant("w0", "hi")
-        top(xa0)
-        top(xa1)
+        quant("w0", "hi", 0, 256)
         mask(xa0)
-        quant("w0", "lo", 128, 256)
+        quant("w0", "lo", 0, 256)
+        top_s(xb0)
+        top_s(xb1)
         rest(xa0)
         mask(xa1)
-        top(xb0)
-        top(xb1)
         mask(xb0)
         rest(xa1)
         rest(xb0)
-        quant("x00", "hi")
+        quant("x00", "hi", 0, 256)
         mask(xb1)
-        quant("x00", "lo")
-        mm(0, 0, 0)
+        quant("x00", "lo", 0, 256)
+        mm(0, 0, 0, 0)
+        mm(0, 0, 0, 1)
+        top_s(wc)
         rest(xb1)
-        quant("x01", "hi")
-        top(wc)
+        quant("x01", "hi", 0, 256)
         mask(wc)
-        quant("x01", "lo")
-        mm(0, 1, 0)
-        relu_s(0, 0, 0)
-        top(xc0)
-        square(0, 0, 0)
-        store_res(0, 0, 0)
+        quant("x01", "lo", 0, 256)
+        mm(0, 1, 0, 0)
+        mm(0, 1, 0, 1)
+        top_s(xc0)
+        top_s(xc1)
         rest(wc)
-        quant("w1", "hi")
+        quant("w1", "hi", 0, 256)
         mask(xc0)
-        quant("w1", "lo")
-        mm(0, 0, 1)
-        mm(0, 1, 1)
+        quant("w1", "lo", 0, 256)
+        mm(0, 0, 1, 0)
+        mm(0, 0, 1, 1)
+        mm(0, 1, 1, 0)
+        mm(0, 1, 1, 1)
+        top_s(xd0)
+        relu_s(0, 0, 0)
+        top_s(xd1)
         relu_s(0, 1, 0)
-        top(xc1)
-        square(0, 1, 0)
+        square_s(0, 0, 0)
+        store_res(0, 0, 0)
+        square_s(0, 1, 0)
         store_res(0, 1, 0)
+        mask(xd0)
         rest(xc0)
-        quant("x10", "hi")
+        rest(xd0)
+        quant("x10", "hi", 0, 256)
         mask(xc1)
-        quant("x10", "lo")
-        mm(1, 0, 0)
-        mm(1, 0, 1)
+        quant("x10", "lo", 0, 256)
+        mm(1, 0, 0, 0)
+        mm(1, 0, 0, 1)
+        mm(1, 0, 1, 0)
+        mm(1, 0, 1, 1)
         relu_s(0, 0, 1)
         relu_s(0, 1, 1)
-        square(0, 0, 1)
+        square_s(0, 0, 1)
         store_res(0, 0, 1)
-        square(0, 1, 1)
+        square_s(0, 1, 1)
         store_res(0, 1, 1)
+        mask(xd1)
         rest(xc1)
-        quant("x11", "hi")
-        cast(0, 0)
-        quant("x11", "lo")
-        mm(1, 1, 0)
-        mm(1, 1, 1)
-        quant_out(0, 0)
-        store_codes(0, 0)
+        rest(xd1)
+        quant("x11", "hi", 0, 256)
+        quant("x11", "lo", 0, 256)
+        mm(1, 1, 0, 0)
+        mm(1, 1, 0, 1)
+        mm(1, 1, 1, 0)
+        mm(1, 1, 1, 1)
         relu_s(1, 0, 0)
         relu_s(1, 0, 1)
-        square(1, 0, 0)
+        cast_v(0, 0, 0, 256)
+        square_v(1, 0, 0)
         store_res(1, 0, 0)
-        cast(0, 1)
-        relu_v(1, 1, 0)
-        quant_out(0, 1)
-        store_codes(0, 1)
-        for q in range(4):
-            store_scales(0, q)
-        square(1, 1, 0)
-        store_res(1, 1, 0)
-        relu_s(1, 1, 1)
-        square(1, 0, 1)
+        quant_out(0, 0, 0, 256)
+        store_codes(0, 0)
+        relu_s(1, 1, 0)
+        square_s(1, 0, 1)
         store_res(1, 0, 1)
-        square(1, 1, 1)
+        square_s(1, 1, 0)
+        store_res(1, 1, 0)
+        cast_v(0, 1, 0, 256)
+        relu_v(1, 1, 1)
+        quant_out(0, 1, 0, 256)
+        store_codes(0, 1)
+        square_s(1, 1, 1)
         store_res(1, 1, 1)
-        cast(1, 0)
-        cast(1, 1)
-        quant_out(1, 0)
+        cast_v(1, 0, 0, 256)
+        cast_v(1, 1, 0, 128)
+        cast_s(1, 1, 128, 256)
+        quant_out(1, 0, 0, 256)
         store_codes(1, 0)
-        quant_out(1, 1)
+        quant_out(1, 1, 0, 128)
+        quant_out(1, 1, 128, 256)
+        store_scales(0, nc.scalar)
         store_codes(1, 1)
-        store_scales(1, 0, nc.scalar)
-        store_scales(1, 1)
-        store_scales(1, 2, nc.scalar)
-        store_scales(1, 3)
+        store_scales(1, nc.scalar)
+        store_scales(2)
+        store_scales(3, nc.scalar)

@@ -35,39 +35,49 @@ def tile_mix_split3_tm_pl_relu2_kernel(tc, w, x, out_0, out_1, out_2):
         codes = {}
         scales = {}
         for key in ("w0", "w1", "x00", "x01", "x10", "x11"):
-            for part in ("hi", "lo"):
-                parts[key, part] = sb.tile([P, 1024], BF16, name="b_%s_%s" % (key, part), align_bytes=64)
-                codes[key, part] = sb.tile([P, 256], I32, name="c_%s_%s" % (key, part), align_bytes=64)
-                scales[key, part] = sb.tile([P, 256], U8, name="s_%s_%s" % (key, part), align_bytes=64)
+            parts[key] = sb.tile([P, 2048], BF16, name="b_" + key, align_bytes=64)
+            codes[key] = sb.tile([P, 512], I32, name="c_" + key, align_bytes=64)
+            scales[key] = sb.tile([P, 512], U8, name="s_" + key, align_bytes=64)
 
         def load(name, rows, c0, c1):
             raw[name] = sb.tile([P, PACK, c1 - c0], F32, name="raw_" + name, align_bytes=64)
             nc.sync.dma_start(out=raw[name][:], in_=rows[:, :, c0:c1])
 
+        tops = {}
+        for key in ("x00", "x01", "x10", "x11"):
+            tops[key] = sb.tile([P, 2, 512], BF16, name="t_" + key, align_bytes=64)
+
         def w_piece(name, key, n0, n1):
             src = raw[name][:].rearrange("p j (c i) -> p c j i", i=2)
             top = raw[name][:].bitcast(BF16).rearrange("p j (c i h) -> p c j i h", i=2, h=2)[:, :, :, :, 1]
-            hi = parts[key, "hi"][:, PACK * n0 : PACK * n1]
-            lo = parts[key, "lo"][:, PACK * n0 : PACK * n1]
+            hi = parts[key][:, PACK * n0 : PACK * n1]
+            lo = parts[key][:, 1024 + PACK * n0 : 1024 + PACK * n1]
+            hv = hi.rearrange("p (c i j) -> p c j i", i=2, j=PACK)
             return (
                 src,
                 top,
-                hi.rearrange("p (c i j) -> p c j i", i=2, j=PACK),
+                hv,
+                hv,
                 lo.rearrange("p (c i j) -> p c j i", i=2, j=PACK),
+                hi.bitcast(I32),
                 hi.bitcast(I32),
             )
 
-        def x_piece(name, key, rp, m0, m1):
+        def x_piece(name, key, rp, mh):
             rs = slice(2 * rp, 2 * rp + 2)
+            ms = slice(256 * mh, 256 * mh + 256)
             src = raw[name][:].rearrange("p j (m r) -> p m j r", r=PACK)[:, :, :, rs]
             top = raw[name][:].bitcast(BF16).rearrange("p j (m r h) -> p m j r h", r=PACK, h=2)[:, :, :, rs, 1]
-            hi = parts[key, "hi"][:].rearrange("p (r e) -> p r e", r=2)[:, :, PACK * m0 : PACK * m1]
-            lo = parts[key, "lo"][:].rearrange("p (r e) -> p r e", r=2)[:, :, PACK * m0 : PACK * m1]
+            t = tops[key][:, mh, :]
+            hi = parts[key][:, 0:1024].rearrange("p (r e) -> p r e", r=2)[:, :, ms]
+            lo = parts[key][:, 1024:2048].rearrange("p (r e) -> p r e", r=2)[:, :, ms]
             return (
                 src,
                 top,
+                t.rearrange("p (r m j) -> p m j r", r=2, j=PACK),
                 hi.rearrange("p r (m j) -> p m j r", j=PACK),
                 lo.rearrange("p r (m j) -> p m j r", j=PACK),
+                t.bitcast(I32).rearrange("p (r e) -> p r e", r=2),
                 hi.bitcast(I32),
             )
 
@@ -78,16 +88,25 @@ def tile_mix_split3_tm_pl_relu2_kernel(tc, w, x, out_0, out_1, out_2):
             nc.vector.tensor_copy(out=piece[2], in_=piece[1])
 
         def mask(piece):
-            nc.vector.tensor_scalar(out=piece[4], in0=piece[4], scalar1=KEEP_HI, scalar2=None, op0=ALU.bitwise_and)
+            nc.vector.tensor_scalar(out=piece[6], in0=piece[5], scalar1=KEEP_HI, scalar2=None, op0=ALU.bitwise_and)
+
+        def mask_both(key):
+            nc.vector.tensor_scalar(
+                out=parts[key][:, 0:1024].bitcast(I32).rearrange("p (r mh e) -> p mh r e", r=2, mh=2),
+                in0=tops[key][:].bitcast(I32).rearrange("p mh (r e) -> p mh r e", r=2),
+                scalar1=KEEP_HI,
+                scalar2=None,
+                op0=ALU.bitwise_and,
+            )
 
         def rest(piece):
-            nc.vector.tensor_tensor(out=piece[3], in0=piece[0], in1=piece[2], op=ALU.subtract)
+            nc.vector.tensor_tensor(out=piece[4], in0=piece[0], in1=piece[3], op=ALU.subtract)
 
-        def quant(key, part, c0=0, c1=256):
+        def quant(key, c0=0, c1=512):
             nc.vector.quantize_mx(
-                out=codes[key, part][:, c0:c1].bitcast(FP8X4),
-                scales=scales[key, part][:, c0:c1],
-                in_=parts[key, part][:, PACK * c0 : PACK * c1],
+                out=codes[key][:, c0:c1].bitcast(FP8X4),
+                scales=scales[key][:, c0:c1],
+                in_=parts[key][:, PACK * c0 : PACK * c1],
             )
 
         acc = {}
@@ -108,14 +127,15 @@ def tile_mix_split3_tm_pl_relu2_kernel(tc, w, x, out_0, out_1, out_2):
         def mm(a, rp, h, r):
             xk = "x%d%d" % (a, rp)
             wk = "w%d" % h
-            cols = slice(r * P, (r + 1) * P)
-            for i, (xp, wp) in enumerate((("hi", "hi"), ("hi", "lo"), ("lo", "hi"))):
+            for i, (xp, wp) in enumerate(((0, 0), (0, 1), (1, 0))):
+                cols = slice(256 * xp + r * P, 256 * xp + (r + 1) * P)
+                wcols = slice(256 * wp, 256 * wp + 256)
                 nc.tensor.matmul_mx(
                     out=acc[a, rp, h][:, r, :],
-                    lhsT=codes[xk, xp][:, cols].bitcast(FP8X4),
-                    lhsT_scale=scales[xk, xp][:, cols],
-                    rhs=codes[wk, wp][:].bitcast(FP8X4),
-                    rhs_scale=scales[wk, wp][:],
+                    lhsT=codes[xk][:, cols].bitcast(FP8X4),
+                    lhsT_scale=scales[xk][:, cols],
+                    rhs=codes[wk][:, wcols].bitcast(FP8X4),
+                    rhs_scale=scales[wk][:, wcols],
                     start=(i == 0),
                     stop=(i == 2),
                 )
@@ -186,106 +206,98 @@ def tile_mix_split3_tm_pl_relu2_kernel(tc, w, x, out_0, out_1, out_2):
         wa = w_piece("wa", "w0", 0, 128)
         wb = w_piece("wb", "w0", 128, 256)
         wc = w_piece("wc", "w1", 0, 256)
-        xa0 = x_piece("xa", "x00", 0, 0, 64)
-        xa1 = x_piece("xa", "x01", 1, 0, 64)
-        xb0 = x_piece("xb", "x00", 0, 64, 128)
-        xb1 = x_piece("xb", "x01", 1, 64, 128)
-        xc0 = x_piece("xc", "x10", 0, 0, 64)
-        xc1 = x_piece("xc", "x11", 1, 0, 64)
-        xd0 = x_piece("xd", "x10", 0, 64, 128)
-        xd1 = x_piece("xd", "x11", 1, 64, 128)
+        xa0 = x_piece("xa", "x00", 0, 0)
+        xa1 = x_piece("xa", "x01", 1, 0)
+        xb0 = x_piece("xb", "x00", 0, 1)
+        xb1 = x_piece("xb", "x01", 1, 1)
+        xc0 = x_piece("xc", "x10", 0, 0)
+        xc1 = x_piece("xc", "x11", 1, 0)
+        xd0 = x_piece("xd", "x10", 0, 1)
+        xd1 = x_piece("xd", "x11", 1, 1)
 
         top_v(wa)
         top_s(wb)
         mask(wa)
         rest(wa)
         mask(wb)
+        rest(wb)
         top_s(xa0)
         top_s(xa1)
-        rest(wb)
-        quant("w0", "hi", 0, 256)
-        mask(xa0)
-        quant("w0", "lo", 0, 256)
         top_s(xb0)
         top_s(xb1)
-        rest(xa0)
-        mask(xa1)
-        mask(xb0)
-        rest(xa1)
-        rest(xb0)
-        quant("x00", "hi", 0, 256)
-        mask(xb1)
-        quant("x00", "lo", 0, 256)
-        mm(0, 0, 0, 0)
-        mm(0, 0, 0, 1)
         top_s(wc)
-        rest(xb1)
-        quant("x01", "hi", 0, 256)
-        mask(wc)
-        quant("x01", "lo", 0, 256)
-        mm(0, 1, 0, 0)
-        mm(0, 1, 0, 1)
         top_s(xc0)
         top_s(xc1)
+        top_s(xd0)
+        top_s(xd1)
+        mask(xa0)
+        quant("w0", 0, 512)
+        mask(xa1)
+        rest(xa0)
+        rest(xa1)
+        mask(xb0)
+        mask(xb1)
+        rest(xb0)
+        mask(wc)
+        quant("x00", 0, 512)
+        mm(0, 0, 0, 0)
+        mm(0, 0, 0, 1)
         rest(wc)
-        quant("w1", "hi", 0, 256)
-        mask(xc0)
-        quant("w1", "lo", 0, 256)
+        rest(xb1)
+        quant("w1", 0, 512)
         mm(0, 0, 1, 0)
         mm(0, 0, 1, 1)
+        mask_both("x10")
+        quant("x01", 0, 512)
+        mm(0, 1, 0, 0)
+        mm(0, 1, 0, 1)
         mm(0, 1, 1, 0)
         mm(0, 1, 1, 1)
-        top_s(xd0)
         relu_s(0, 0, 0)
-        top_s(xd1)
-        relu_s(0, 1, 0)
         square_s(0, 0, 0)
         store_res(0, 0, 0)
+        relu_s(0, 0, 1)
+        square_s(0, 0, 1)
+        store_res(0, 0, 1)
+        relu_s(0, 1, 0)
+        relu_s(0, 1, 1)
         square_s(0, 1, 0)
         store_res(0, 1, 0)
-        mask(xd0)
+        square_s(0, 1, 1)
+        store_res(0, 1, 1)
         rest(xc0)
+        mask_both("x11")
         rest(xd0)
-        quant("x10", "hi", 0, 256)
-        mask(xc1)
-        quant("x10", "lo", 0, 256)
+        rest(xc1)
+        quant("x10", 0, 512)
         mm(1, 0, 0, 0)
         mm(1, 0, 0, 1)
         mm(1, 0, 1, 0)
         mm(1, 0, 1, 1)
-        relu_s(0, 0, 1)
-        relu_s(0, 1, 1)
-        square_s(0, 0, 1)
-        store_res(0, 0, 1)
-        square_s(0, 1, 1)
-        store_res(0, 1, 1)
-        mask(xd1)
-        rest(xc1)
         rest(xd1)
-        quant("x11", "hi", 0, 256)
-        quant("x11", "lo", 0, 256)
+        quant("x11", 0, 512)
         mm(1, 1, 0, 0)
         mm(1, 1, 0, 1)
         mm(1, 1, 1, 0)
         mm(1, 1, 1, 1)
         relu_s(1, 0, 0)
         relu_s(1, 0, 1)
+        square_s(1, 0, 0)
+        square_s(1, 0, 1)
         cast_v(0, 0, 0, 256)
-        square_v(1, 0, 0)
-        store_res(1, 0, 0)
+        cast_v(0, 1, 0, 256)
         quant_out(0, 0, 0, 256)
         store_codes(0, 0)
-        relu_s(1, 1, 0)
-        square_s(1, 0, 1)
+        store_res(1, 0, 0)
         store_res(1, 0, 1)
+        relu_v(1, 1, 0)
+        relu_v(1, 1, 1)
         square_s(1, 1, 0)
         store_res(1, 1, 0)
-        cast_v(0, 1, 0, 256)
-        relu_v(1, 1, 1)
         quant_out(0, 1, 0, 256)
-        store_codes(0, 1)
         square_s(1, 1, 1)
         store_res(1, 1, 1)
+        store_codes(0, 1)
         cast_v(1, 0, 0, 256)
         cast_v(1, 1, 0, 128)
         cast_s(1, 1, 128, 256)

@@ -15,298 +15,302 @@ ALU = mybir.AluOpType
 
 P = 128
 PACK = 4
-HALF_N = 256
+HI, LO = 0, 1
+HALF = M // 2
+QUARTER = M // 4
+GROUPS = T // (P * PACK)
 KEEP_HI = -983056
 
 
 def tile_mix_split3_tm_pl_relu2_kernel(tc, w, x, out_0, out_1, out_2):
     nc = tc.nc
     with ExitStack() as ctx:
-        sb = ctx.enter_context(tc.tile_pool(name="sb", bufs=1))
-        ps = ctx.enter_context(tc.psum_pool(name="ps", bufs=1))
+        sbuf = ctx.enter_context(tc.tile_pool(name="sbuf", bufs=1))
+        psum = ctx.enter_context(tc.psum_pool(name="psum", bufs=1))
         ctx.enter_context(tc.manual_schedule())
+
+        def tile(name, shape, dtype):
+            return sbuf.tile([P] + shape, dtype, name=name, align_bytes=64)
 
         w_rows = w.rearrange("(p j) n -> p j n", j=PACK)
         x_rows = x.rearrange("(p j) t -> p j t", j=PACK)
-        out_rows = out_0.rearrange("(a p r) n -> a p r n", a=2, r=PACK)
+        w_raw = {}
+        x_raw = {}
 
-        raw = {}
-        parts = {}
-        codes = {}
-        scales = {}
-        for key in ("w0", "w1", "x00", "x01", "x10", "x11"):
-            parts[key] = sb.tile([P, 2048], BF16, name="b_" + key, align_bytes=64)
-            codes[key] = sb.tile([P, 512], I32, name="c_" + key, align_bytes=64)
-            scales[key] = sb.tile([P, 512], U8, name="s_" + key, align_bytes=64)
+        def load_w(n0, n1):
+            w_raw[n0, n1] = tile("w_raw_%d" % n0, [PACK, n1 - n0], F32)
+            nc.sync.dma_start(out=w_raw[n0, n1][:], in_=w_rows[:, :, n0:n1])
 
-        def load(name, rows, c0, c1):
-            raw[name] = sb.tile([P, PACK, c1 - c0], F32, name="raw_" + name, align_bytes=64)
-            nc.sync.dma_start(out=raw[name][:], in_=rows[:, :, c0:c1])
+        def load_x(a, half):
+            t0 = (2 * a + half) * HALF
+            x_raw[a, half] = tile("x_raw_%d_%d" % (a, half), [PACK, HALF], F32)
+            nc.sync.dma_start(out=x_raw[a, half][:], in_=x_rows[:, :, t0 : t0 + HALF])
 
-        tops = {}
-        for key in ("x00", "x01", "x10", "x11"):
-            tops[key] = sb.tile([P, 2, 512], BF16, name="t_" + key, align_bytes=64)
+        load_w(0, QUARTER)
+        load_w(QUARTER, HALF)
+        load_x(0, 0)
+        load_x(0, 1)
+        load_w(HALF, M)
+        load_x(1, 0)
+        load_x(1, 1)
 
-        def w_piece(name, key, n0, n1):
-            src = raw[name][:].rearrange("p j (c i) -> p c j i", i=2)
-            top = raw[name][:].bitcast(BF16).rearrange("p j (c i h) -> p c j i h", i=2, h=2)[:, :, :, :, 1]
-            hi = parts[key][:, PACK * n0 : PACK * n1]
-            lo = parts[key][:, 1024 + PACK * n0 : 1024 + PACK * n1]
-            hv = hi.rearrange("p (c i j) -> p c j i", i=2, j=PACK)
-            return (
-                src,
-                top,
-                hv,
-                hv,
-                lo.rearrange("p (c i j) -> p c j i", i=2, j=PACK),
-                hi.bitcast(I32),
-                hi.bitcast(I32),
+        w_parts = tile("w_parts", [2, M * PACK], BF16)
+        w_codes = tile("w_codes", [2, M], I32)
+        w_scales = tile("w_scales", [2, M], U8)
+        x_upper = {}
+        x_parts = {}
+        x_codes = {}
+        x_scales = {}
+        for a in range(GROUPS):
+            for pair in range(2):
+                x_upper[a, pair] = tile("x_upper_%d_%d" % (a, pair), [2, P * PACK], BF16)
+                x_parts[a, pair] = tile("x_parts_%d_%d" % (a, pair), [2, 2 * P * PACK], BF16)
+                x_codes[a, pair] = tile("x_codes_%d_%d" % (a, pair), [2, 2 * P], I32)
+                x_scales[a, pair] = tile("x_scales_%d_%d" % (a, pair), [2, 2 * P], U8)
+
+        def w_view(part, n0, n1):
+            return w_parts[:, part, PACK * n0 : PACK * n1].rearrange("p (c i j) -> p c j i", i=2, j=PACK)
+
+        def upper_w(copy, n0, n1):
+            halves = w_raw[n0, n1][:].bitcast(BF16).rearrange("p j (c i u) -> p c j i u", i=2, u=2)
+            copy(out=w_view(HI, n0, n1), in_=halves[:, :, :, :, 1])
+
+        def mask_w(n0, n1):
+            words = w_parts[:, HI, PACK * n0 : PACK * n1].bitcast(I32)
+            nc.vector.tensor_scalar(out=words, in0=words, scalar1=KEEP_HI, scalar2=None, op0=ALU.bitwise_and)
+
+        def subtract_w(n0, n1):
+            nc.vector.tensor_tensor(
+                out=w_view(LO, n0, n1),
+                in0=w_raw[n0, n1][:].rearrange("p j (c i) -> p c j i", i=2),
+                in1=w_view(HI, n0, n1),
+                op=ALU.subtract,
             )
 
-        def x_piece(name, key, rp, mh):
-            rs = slice(2 * rp, 2 * rp + 2)
-            ms = slice(256 * mh, 256 * mh + 256)
-            src = raw[name][:].rearrange("p j (m r) -> p m j r", r=PACK)[:, :, :, rs]
-            top = raw[name][:].bitcast(BF16).rearrange("p j (m r h) -> p m j r h", r=PACK, h=2)[:, :, :, rs, 1]
-            t = tops[key][:, mh, :]
-            hi = parts[key][:, 0:1024].rearrange("p (r e) -> p r e", r=2)[:, :, ms]
-            lo = parts[key][:, 1024:2048].rearrange("p (r e) -> p r e", r=2)[:, :, ms]
-            return (
-                src,
-                top,
-                t.rearrange("p (r m j) -> p m j r", r=2, j=PACK),
-                hi.rearrange("p r (m j) -> p m j r", j=PACK),
-                lo.rearrange("p r (m j) -> p m j r", j=PACK),
-                t.bitcast(I32).rearrange("p (r e) -> p r e", r=2),
-                hi.bitcast(I32),
+        def quantize_w(part, n0, n1):
+            nc.vector.quantize_mx(
+                out=w_codes[:, part, n0:n1].bitcast(FP8X4),
+                scales=w_scales[:, part, n0:n1],
+                in_=w_parts[:, part, PACK * n0 : PACK * n1],
             )
 
-        def top_s(piece):
-            nc.scalar.copy(out=piece[2], in_=piece[1])
+        def x_view(a, pair, part, half):
+            slots = x_parts[a, pair][:, part, :].rearrange("p (r h m j) -> p h m j r", r=2, h=2, j=PACK)
+            return slots[:, half, :, :, :]
 
-        def top_v(piece):
-            nc.vector.tensor_copy(out=piece[2], in_=piece[1])
+        def upper_x(a, pair, half):
+            halves = x_raw[a, half][:].bitcast(BF16).rearrange("p j (m r u) -> p m j r u", r=PACK, u=2)
+            nc.scalar.copy(
+                out=x_upper[a, pair][:, half, :].rearrange("p (r m j) -> p m j r", r=2, j=PACK),
+                in_=halves[:, :, :, 2 * pair : 2 * pair + 2, 1],
+            )
 
-        def mask(piece):
-            nc.vector.tensor_scalar(out=piece[6], in0=piece[5], scalar1=KEEP_HI, scalar2=None, op0=ALU.bitwise_and)
-
-        def mask_both(key):
+        def mask_x(a, pair, h0, h1):
+            words = x_parts[a, pair][:, HI, :].bitcast(I32).rearrange("p (r h e) -> p h r e", r=2, h=2)
             nc.vector.tensor_scalar(
-                out=parts[key][:, 0:1024].bitcast(I32).rearrange("p (r mh e) -> p mh r e", r=2, mh=2),
-                in0=tops[key][:].bitcast(I32).rearrange("p mh (r e) -> p mh r e", r=2),
+                out=words[:, h0:h1, :, :],
+                in0=x_upper[a, pair][:, h0:h1, :].bitcast(I32).rearrange("p h (r e) -> p h r e", r=2),
                 scalar1=KEEP_HI,
                 scalar2=None,
                 op0=ALU.bitwise_and,
             )
 
-        def rest(piece):
-            nc.vector.tensor_tensor(out=piece[4], in0=piece[0], in1=piece[3], op=ALU.subtract)
+        def subtract_x(a, pair, half):
+            values = x_raw[a, half][:].rearrange("p j (m r) -> p m j r", r=PACK)
+            nc.vector.tensor_tensor(
+                out=x_view(a, pair, LO, half),
+                in0=values[:, :, :, 2 * pair : 2 * pair + 2],
+                in1=x_view(a, pair, HI, half),
+                op=ALU.subtract,
+            )
 
-        def quant(key, c0=0, c1=512):
+        def quantize_x(a, pair, part):
             nc.vector.quantize_mx(
-                out=codes[key][:, c0:c1].bitcast(FP8X4),
-                scales=scales[key][:, c0:c1],
-                in_=parts[key][:, PACK * c0 : PACK * c1],
+                out=x_codes[a, pair][:, part, :].bitcast(FP8X4),
+                scales=x_scales[a, pair][:, part, :],
+                in_=x_parts[a, pair][:, part, :],
             )
 
         acc = {}
         relu = {}
-        res = {}
-        res16 = {}
+        result = {}
+        result_bf16 = {}
         out_codes = {}
-        out_scales = sb.tile([P, 2, M], U8, name="out_scales", align_bytes=64)
-        for a in range(2):
-            for h in range(2):
-                res[a, h] = sb.tile([P, PACK, HALF_N], F32, name="res_%d_%d" % (a, h), align_bytes=64)
-                res16[a, h] = sb.tile([P, PACK * HALF_N], BF16, name="res16_%d_%d" % (a, h), align_bytes=64)
-                out_codes[a, h] = sb.tile([P, HALF_N], I32, name="oc_%d_%d" % (a, h), align_bytes=64)
-                for rp in range(2):
-                    acc[a, rp, h] = ps.tile([P, 2, HALF_N], F32, name="acc_%d_%d_%d" % (a, rp, h))
-                    relu[a, rp, h] = sb.tile([P, 2, HALF_N], F32, name="relu_%d_%d_%d" % (a, rp, h), align_bytes=64)
+        for a in range(GROUPS):
+            result[a] = tile("result_%d" % a, [PACK, M], F32)
+            result_bf16[a] = tile("result_bf16_%d" % a, [M * PACK], BF16)
+            out_codes[a] = tile("out_codes_%d" % a, [M], I32)
+            for b in range(PACK):
+                acc[a, b] = psum.tile([P, M], F32, name="acc_%d_%d" % (a, b))
+                relu[a, b] = tile("relu_%d_%d" % (a, b), [M], F32)
+        out_scales = tile("out_scales", [GROUPS, M], U8)
 
-        def mm(a, rp, h, r):
-            xk = "x%d%d" % (a, rp)
-            wk = "w%d" % h
-            for i, (xp, wp) in enumerate(((0, 0), (0, 1), (1, 0))):
-                cols = slice(256 * xp + r * P, 256 * xp + (r + 1) * P)
-                wcols = slice(256 * wp, 256 * wp + 256)
+        def passes(out, a, r, n0, n1, products):
+            m_cols = slice((r % 2) * P, (r % 2 + 1) * P)
+            for x_part, w_part in products:
                 nc.tensor.matmul_mx(
-                    out=acc[a, rp, h][:, r, :],
-                    lhsT=codes[xk][:, cols].bitcast(FP8X4),
-                    lhsT_scale=scales[xk][:, cols],
-                    rhs=codes[wk][:, wcols].bitcast(FP8X4),
-                    rhs_scale=scales[wk][:, wcols],
-                    start=(i == 0),
-                    stop=(i == 2),
+                    out=out,
+                    lhsT=x_codes[a, r // 2][:, x_part, m_cols].bitcast(FP8X4),
+                    lhsT_scale=x_scales[a, r // 2][:, x_part, m_cols],
+                    rhs=w_codes[:, w_part, n0:n1].bitcast(FP8X4),
+                    rhs_scale=w_scales[:, w_part, n0:n1],
+                    start=(x_part, w_part) == (HI, HI),
+                    stop=x_part == LO,
                 )
 
-        def relu_s(a, rp, h):
-            nc.scalar.activation(out=relu[a, rp, h][:], in_=acc[a, rp, h][:], func=ACT.Relu)
+        def multiply_half(h):
+            for r in range(2):
+                out = acc[0, h][:, r * HALF : (r + 1) * HALF]
+                passes(out, 0, r, h * HALF, (h + 1) * HALF, [(HI, HI), (HI, LO), (LO, HI)])
 
-        def relu_v(a, rp, h):
-            nc.vector.tensor_scalar(out=relu[a, rp, h][:], in0=acc[a, rp, h][:], scalar1=0.0, scalar2=None, op0=ALU.max)
+        def multiply_hi(a, pair):
+            for r in (2 * pair, 2 * pair + 1):
+                passes(acc[a, r][:], a, r, 0, M, [(HI, HI), (HI, LO)])
 
-        def square_s(a, rp, h):
-            nc.scalar.activation(out=res[a, h][:, 2 * rp : 2 * rp + 2, :], in_=relu[a, rp, h][:], func=ACT.Square)
+        def multiply_lo(a, pair):
+            for r in (2 * pair, 2 * pair + 1):
+                passes(acc[a, r][:], a, r, 0, M, [(LO, HI)])
 
-        def square_v(a, rp, h):
-            nc.vector.tensor_tensor(
-                out=res[a, h][:, 2 * rp : 2 * rp + 2, :], in0=relu[a, rp, h][:], in1=relu[a, rp, h][:], op=ALU.mult
+        def relu_scalar(a, b):
+            nc.scalar.activation(out=relu[a, b][:], in_=acc[a, b][:], func=ACT.Relu)
+
+        def relu_vector(a, b):
+            nc.vector.tensor_scalar(out=relu[a, b][:], in0=acc[a, b][:], scalar1=0.0, scalar2=None, op0=ALU.max)
+
+        def square_half(h):
+            nc.scalar.activation(
+                out=result[0][:, 0:2, h * HALF : (h + 1) * HALF],
+                in_=relu[0, h][:].rearrange("p (r n) -> p r n", r=2),
+                func=ACT.Square,
             )
 
-        def store_res(a, rp, h, eng=nc.sync):
-            eng.dma_start(
-                out=out_rows[a][:, 2 * rp : 2 * rp + 2, h * HALF_N : (h + 1) * HALF_N],
-                in_=res[a, h][:, 2 * rp : 2 * rp + 2, :],
+        def square_scalar(a, r):
+            nc.scalar.activation(out=result[a][:, r, :], in_=relu[a, r][:], func=ACT.Square)
+
+        def square_vector(a, r):
+            nc.vector.tensor_tensor(out=result[a][:, r, :], in0=relu[a, r][:], in1=relu[a, r][:], op=ALU.mult)
+
+        out_rows = out_0.rearrange("(a p r) n -> a p r n", a=GROUPS, r=PACK)
+
+        def store_result(a, r0, r1):
+            nc.sync.dma_start(out=out_rows[a][:, r0:r1, :], in_=result[a][:, r0:r1, :])
+
+        def round_result(copy, a, n0, n1):
+            copy(
+                out=result_bf16[a][:, PACK * n0 : PACK * n1].rearrange("p (c i r) -> p c r i", i=2, r=PACK),
+                in_=result[a][:, :, n0:n1].rearrange("p r (c i) -> p c r i", i=2),
             )
 
-        def cast_views(a, h, c0, c1):
-            dst = res16[a, h][:, PACK * c0 : PACK * c1].rearrange("p (c i r) -> p c r i", i=2, r=PACK)
-            src = res[a, h][:, :, c0:c1].rearrange("p r (c i) -> p c r i", i=2)
-            return dst, src
-
-        def cast_v(a, h, c0, c1):
-            dst, src = cast_views(a, h, c0, c1)
-            nc.vector.tensor_copy(out=dst, in_=src)
-
-        def cast_s(a, h, c0, c1):
-            dst, src = cast_views(a, h, c0, c1)
-            nc.scalar.copy(out=dst, in_=src)
-
-        def quant_out(a, h, c0, c1):
+        def quantize_result(a, n0, n1):
             nc.vector.quantize_mx(
-                out=out_codes[a, h][:, c0:c1].bitcast(FP8X4),
-                scales=out_scales[:, a, h * HALF_N + c0 : h * HALF_N + c1],
-                in_=res16[a, h][:, PACK * c0 : PACK * c1],
+                out=out_codes[a][:, n0:n1].bitcast(FP8X4),
+                scales=out_scales[:, a, n0:n1],
+                in_=result_bf16[a][:, PACK * n0 : PACK * n1],
             )
 
-        def store_codes(a, h, eng=nc.sync):
+        def store_codes(a, n0, n1):
             words = out_1[a].rearrange("p n i -> p (n i)").bitcast(I32)
-            eng.dma_start(out=words[:, h * HALF_N : (h + 1) * HALF_N], in_=out_codes[a, h][:])
+            nc.sync.dma_start(out=words[:, n0:n1], in_=out_codes[a][:, n0:n1])
 
-        def store_scales(q, eng=nc.sync):
-            eng.dma_start(
-                out=out_2[:, 4 * q : 4 * q + 4, :].rearrange("a q n -> q a n").bitcast(I32),
+        def store_scales(queue, q):
+            queue.dma_start(
+                out=out_2[:, 4 * q : 4 * q + 4, :].rearrange("a b n -> b a n").bitcast(I32),
                 in_=out_scales[32 * q : 32 * q + 4, :, :].bitcast(I32),
             )
 
-        load("wa", w_rows, 0, 128)
-        load("wb", w_rows, 128, 256)
-        load("xa", x_rows, 0, 256)
-        load("xb", x_rows, 256, 512)
-        load("wc", w_rows, 256, 512)
-        load("xc", x_rows, 512, 768)
-        load("xd", x_rows, 768, 1024)
+        on_vector = nc.vector.tensor_copy
+        on_scalar = nc.scalar.copy
 
-        warm = sb.tile([P, 1], F32, name="warm")
-        nc.gpsimd.memset(warm[:], 0.0)
-        warm_out = sb.tile([P, 1], F32, name="warm_out")
-        nc.scalar.activation(out=warm_out[:], in_=warm[:], func=ACT.Square)
+        upper_w(on_vector, 0, QUARTER)
+        upper_w(on_scalar, QUARTER, HALF)
+        for half in range(2):
+            for pair in range(2):
+                upper_x(0, pair, half)
+        upper_w(on_scalar, HALF, M)
+        for half in range(2):
+            for pair in range(2):
+                upper_x(1, pair, half)
 
-        wa = w_piece("wa", "w0", 0, 128)
-        wb = w_piece("wb", "w0", 128, 256)
-        wc = w_piece("wc", "w1", 0, 256)
-        xa0 = x_piece("xa", "x00", 0, 0)
-        xa1 = x_piece("xa", "x01", 1, 0)
-        xb0 = x_piece("xb", "x00", 0, 1)
-        xb1 = x_piece("xb", "x01", 1, 1)
-        xc0 = x_piece("xc", "x10", 0, 0)
-        xc1 = x_piece("xc", "x11", 1, 0)
-        xd0 = x_piece("xd", "x10", 0, 1)
-        xd1 = x_piece("xd", "x11", 1, 1)
+        mask_w(0, QUARTER)
+        mask_w(QUARTER, HALF)
+        subtract_w(0, QUARTER)
+        subtract_w(QUARTER, HALF)
+        mask_x(0, 0, 0, 1)
+        quantize_w(HI, 0, HALF)
+        subtract_x(0, 0, 0)
+        quantize_w(LO, 0, HALF)
+        mask_x(0, 0, 1, 2)
+        mask_x(0, 1, 0, 2)
+        subtract_x(0, 0, 1)
+        quantize_x(0, 0, HI)
+        quantize_x(0, 0, LO)
+        multiply_half(0)
 
-        top_v(wa)
-        top_s(wb)
-        mask(wa)
-        rest(wa)
-        mask(wb)
-        rest(wb)
-        top_s(xa0)
-        top_s(xa1)
-        top_s(xb0)
-        top_s(xb1)
-        top_s(wc)
-        top_s(xc0)
-        top_s(xc1)
-        top_s(xd0)
-        top_s(xd1)
-        mask(xa0)
-        quant("w0", 0, 512)
-        mask(xa1)
-        rest(xa0)
-        rest(xa1)
-        mask(xb0)
-        mask(xb1)
-        rest(xb0)
-        mask(wc)
-        quant("x00", 0, 512)
-        mm(0, 0, 0, 0)
-        mm(0, 0, 0, 1)
-        rest(wc)
-        rest(xb1)
-        quant("w1", 0, 512)
-        mm(0, 0, 1, 0)
-        mm(0, 0, 1, 1)
-        mask_both("x10")
-        quant("x01", 0, 512)
-        mm(0, 1, 0, 0)
-        mm(0, 1, 0, 1)
-        mm(0, 1, 1, 0)
-        mm(0, 1, 1, 1)
-        relu_s(0, 0, 0)
-        square_s(0, 0, 0)
-        store_res(0, 0, 0)
-        relu_s(0, 0, 1)
-        square_s(0, 0, 1)
-        store_res(0, 0, 1)
-        relu_s(0, 1, 0)
-        relu_s(0, 1, 1)
-        square_s(0, 1, 0)
-        store_res(0, 1, 0)
-        square_s(0, 1, 1)
-        store_res(0, 1, 1)
-        rest(xc0)
-        mask_both("x11")
-        rest(xd0)
-        rest(xc1)
-        quant("x10", 0, 512)
-        mm(1, 0, 0, 0)
-        mm(1, 0, 0, 1)
-        mm(1, 0, 1, 0)
-        mm(1, 0, 1, 1)
-        rest(xd1)
-        quant("x11", 0, 512)
-        mm(1, 1, 0, 0)
-        mm(1, 1, 0, 1)
-        mm(1, 1, 1, 0)
-        mm(1, 1, 1, 1)
-        relu_s(1, 0, 0)
-        relu_s(1, 0, 1)
-        square_s(1, 0, 0)
-        square_s(1, 0, 1)
-        cast_v(0, 0, 0, 256)
-        cast_v(0, 1, 0, 256)
-        quant_out(0, 0, 0, 256)
-        store_codes(0, 0)
-        store_res(1, 0, 0)
-        store_res(1, 0, 1)
-        relu_v(1, 1, 0)
-        relu_v(1, 1, 1)
-        square_s(1, 1, 0)
-        store_res(1, 1, 0)
-        quant_out(0, 1, 0, 256)
-        square_s(1, 1, 1)
-        store_res(1, 1, 1)
-        store_codes(0, 1)
-        cast_v(1, 0, 0, 256)
-        cast_v(1, 1, 0, 128)
-        cast_s(1, 1, 128, 256)
-        quant_out(1, 0, 0, 256)
-        store_codes(1, 0)
-        quant_out(1, 1, 0, 128)
-        quant_out(1, 1, 128, 256)
-        store_scales(0, nc.scalar)
-        store_codes(1, 1)
-        store_scales(1, nc.scalar)
-        store_scales(2)
-        store_scales(3, nc.scalar)
+        mask_w(HALF, M)
+        quantize_x(0, 1, HI)
+        subtract_w(HALF, M)
+        quantize_w(HI, HALF, M)
+        quantize_w(LO, HALF, M)
+        multiply_half(1)
+        multiply_hi(0, 1)
+        relu_scalar(0, 0)
+        relu_scalar(0, 1)
+        square_half(0)
+        square_half(1)
+        store_result(0, 0, 2)
+
+        subtract_x(0, 1, 0)
+        mask_x(1, 0, 0, 2)
+        subtract_x(0, 1, 1)
+        quantize_x(1, 0, HI)
+        subtract_x(1, 0, 0)
+        quantize_x(0, 1, LO)
+        multiply_lo(0, 1)
+        multiply_hi(1, 0)
+        relu_scalar(0, 2)
+        relu_scalar(0, 3)
+        square_scalar(0, 2)
+        store_result(0, 2, 3)
+        subtract_x(1, 0, 1)
+        mask_x(1, 1, 0, 2)
+        quantize_x(1, 0, LO)
+        multiply_lo(1, 0)
+
+        subtract_x(1, 1, 0)
+        quantize_x(1, 1, HI)
+        multiply_hi(1, 1)
+        subtract_x(1, 1, 1)
+        square_vector(0, 3)
+        store_result(0, 3, 4)
+        quantize_x(1, 1, LO)
+        multiply_lo(1, 1)
+
+        relu_scalar(1, 0)
+        relu_scalar(1, 1)
+        square_scalar(1, 0)
+        store_result(1, 0, 1)
+        square_scalar(1, 1)
+        store_result(1, 1, 2)
+        round_result(on_vector, 0, 0, HALF)
+        relu_vector(1, 2)
+        quantize_result(0, 0, HALF)
+        square_vector(1, 2)
+        store_result(1, 2, 3)
+        relu_scalar(1, 3)
+        square_scalar(1, 3)
+        store_result(1, 3, 4)
+        round_result(on_vector, 0, HALF, M)
+        round_result(on_scalar, 1, 0, QUARTER)
+        round_result(on_vector, 1, QUARTER, HALF)
+        quantize_result(0, HALF, M)
+        store_codes(0, 0, M)
+        round_result(on_scalar, 1, HALF, HALF + QUARTER)
+        round_result(on_vector, 1, HALF + QUARTER, M)
+        quantize_result(1, 0, HALF)
+        store_codes(1, 0, HALF)
+        quantize_result(1, HALF, M)
+        store_scales(nc.scalar, 0)
+        store_scales(nc.sync, 1)
+        store_scales(nc.scalar, 2)
+        store_codes(1, HALF, M)
+        store_scales(nc.sync, 3)

from contextlib import ExitStack

import concourse.mybir as mybir

K, M, T = 512, 512, 1024
FLOPS = 3 * 2 * K * M * T

F32 = mybir.dt.float32
BF16 = mybir.dt.bfloat16
I32 = mybir.dt.int32
U8 = mybir.dt.uint8
FP8X4 = mybir.dt.float8_e4m3fn_x4
ACT = mybir.ActivationFunctionType
ALU = mybir.AluOpType

P = 128
PACK = 4
HI, LO = 0, 1
HALF = M // 2
QUARTER = M // 4
GROUPS = T // (P * PACK)
KEEP_HI = -983056


def tile_mix_split3_tm_pl_relu2_kernel(tc, w, x, out_0, out_1, out_2):
    nc = tc.nc
    with ExitStack() as ctx:
        sbuf = ctx.enter_context(tc.tile_pool(name="sbuf", bufs=1))
        psum = ctx.enter_context(tc.psum_pool(name="psum", bufs=1))
        ctx.enter_context(tc.manual_schedule())

        def tile(name, shape, dtype):
            return sbuf.tile([P] + shape, dtype, name=name, align_bytes=64)

        w_rows = w.rearrange("(p j) n -> p j n", j=PACK)
        x_rows = x.rearrange("(p j) t -> p j t", j=PACK)
        w_raw = {}
        x_raw = {}

        def load_w(n0, n1):
            w_raw[n0, n1] = tile("w_raw_%d" % n0, [PACK, n1 - n0], F32)
            nc.sync.dma_start(out=w_raw[n0, n1][:], in_=w_rows[:, :, n0:n1])

        def load_x(a, half):
            t0 = (2 * a + half) * HALF
            x_raw[a, half] = tile("x_raw_%d_%d" % (a, half), [PACK, HALF], F32)
            nc.sync.dma_start(out=x_raw[a, half][:], in_=x_rows[:, :, t0 : t0 + HALF])

        load_w(0, QUARTER)
        load_w(QUARTER, HALF)
        load_x(0, 0)
        load_x(0, 1)
        load_w(HALF, M)
        load_x(1, 0)
        load_x(1, 1)

        w_parts = tile("w_parts", [2, M * PACK], BF16)
        w_codes = tile("w_codes", [2, M], I32)
        w_scales = tile("w_scales", [2, M], U8)
        x_upper = {}
        x_parts = {}
        x_codes = {}
        x_scales = {}
        for a in range(GROUPS):
            for pair in range(2):
                x_upper[a, pair] = tile("x_upper_%d_%d" % (a, pair), [2, P * PACK], BF16)
                x_parts[a, pair] = tile("x_parts_%d_%d" % (a, pair), [2, 2 * P * PACK], BF16)
                x_codes[a, pair] = tile("x_codes_%d_%d" % (a, pair), [2, 2 * P], I32)
                x_scales[a, pair] = tile("x_scales_%d_%d" % (a, pair), [2, 2 * P], U8)

        def w_view(part, n0, n1):
            return w_parts[:, part, PACK * n0 : PACK * n1].rearrange("p (c i j) -> p c j i", i=2, j=PACK)

        def upper_w(copy, n0, n1):
            halves = w_raw[n0, n1][:].bitcast(BF16).rearrange("p j (c i u) -> p c j i u", i=2, u=2)
            copy(out=w_view(HI, n0, n1), in_=halves[:, :, :, :, 1])

        def mask_w(n0, n1):
            words = w_parts[:, HI, PACK * n0 : PACK * n1].bitcast(I32)
            nc.vector.tensor_scalar(out=words, in0=words, scalar1=KEEP_HI, scalar2=None, op0=ALU.bitwise_and)

        def subtract_w(n0, n1):
            nc.vector.tensor_tensor(
                out=w_view(LO, n0, n1),
                in0=w_raw[n0, n1][:].rearrange("p j (c i) -> p c j i", i=2),
                in1=w_view(HI, n0, n1),
                op=ALU.subtract,
            )

        def quantize_w(part, n0, n1):
            nc.vector.quantize_mx(
                out=w_codes[:, part, n0:n1].bitcast(FP8X4),
                scales=w_scales[:, part, n0:n1],
                in_=w_parts[:, part, PACK * n0 : PACK * n1],
            )

        def x_view(a, pair, part, half):
            slots = x_parts[a, pair][:, part, :].rearrange("p (r h m j) -> p h m j r", r=2, h=2, j=PACK)
            return slots[:, half, :, :, :]

        def upper_x(a, pair, half):
            halves = x_raw[a, half][:].bitcast(BF16).rearrange("p j (m r u) -> p m j r u", r=PACK, u=2)
            nc.scalar.copy(
                out=x_upper[a, pair][:, half, :].rearrange("p (r m j) -> p m j r", r=2, j=PACK),
                in_=halves[:, :, :, 2 * pair : 2 * pair + 2, 1],
            )

        def mask_x(a, pair, h0, h1):
            words = x_parts[a, pair][:, HI, :].bitcast(I32).rearrange("p (r h e) -> p h r e", r=2, h=2)
            nc.vector.tensor_scalar(
                out=words[:, h0:h1, :, :],
                in0=x_upper[a, pair][:, h0:h1, :].bitcast(I32).rearrange("p h (r e) -> p h r e", r=2),
                scalar1=KEEP_HI,
                scalar2=None,
                op0=ALU.bitwise_and,
            )

        def subtract_x(a, pair, half):
            values = x_raw[a, half][:].rearrange("p j (m r) -> p m j r", r=PACK)
            nc.vector.tensor_tensor(
                out=x_view(a, pair, LO, half),
                in0=values[:, :, :, 2 * pair : 2 * pair + 2],
                in1=x_view(a, pair, HI, half),
                op=ALU.subtract,
            )

        def quantize_x(a, pair, part):
            nc.vector.quantize_mx(
                out=x_codes[a, pair][:, part, :].bitcast(FP8X4),
                scales=x_scales[a, pair][:, part, :],
                in_=x_parts[a, pair][:, part, :],
            )

        acc = {}
        relu = {}
        result = {}
        result_bf16 = {}
        out_codes = {}
        for a in range(GROUPS):
            result[a] = tile("result_%d" % a, [PACK, M], F32)
            result_bf16[a] = tile("result_bf16_%d" % a, [M * PACK], BF16)
            out_codes[a] = tile("out_codes_%d" % a, [M], I32)
            for b in range(PACK):
                acc[a, b] = psum.tile([P, M], F32, name="acc_%d_%d" % (a, b))
                relu[a, b] = tile("relu_%d_%d" % (a, b), [M], F32)
        out_scales = tile("out_scales", [GROUPS, M], U8)

        def passes(out, a, r, n0, n1, products):
            m_cols = slice((r % 2) * P, (r % 2 + 1) * P)
            for x_part, w_part in products:
                nc.tensor.matmul_mx(
                    out=out,
                    lhsT=x_codes[a, r // 2][:, x_part, m_cols].bitcast(FP8X4),
                    lhsT_scale=x_scales[a, r // 2][:, x_part, m_cols],
                    rhs=w_codes[:, w_part, n0:n1].bitcast(FP8X4),
                    rhs_scale=w_scales[:, w_part, n0:n1],
                    start=(x_part, w_part) == (HI, HI),
                    stop=x_part == LO,
                )

        def multiply_half(h):
            for r in range(2):
                out = acc[0, h][:, r * HALF : (r + 1) * HALF]
                passes(out, 0, r, h * HALF, (h + 1) * HALF, [(HI, HI), (HI, LO), (LO, HI)])

        def multiply_hi(a, pair):
            for r in (2 * pair, 2 * pair + 1):
                passes(acc[a, r][:], a, r, 0, M, [(HI, HI), (HI, LO)])

        def multiply_lo(a, pair):
            for r in (2 * pair, 2 * pair + 1):
                passes(acc[a, r][:], a, r, 0, M, [(LO, HI)])

        def relu_scalar(a, b):
            nc.scalar.activation(out=relu[a, b][:], in_=acc[a, b][:], func=ACT.Relu)

        def relu_vector(a, b):
            nc.vector.tensor_scalar(out=relu[a, b][:], in0=acc[a, b][:], scalar1=0.0, scalar2=None, op0=ALU.max)

        def square_half(h):
            nc.scalar.activation(
                out=result[0][:, 0:2, h * HALF : (h + 1) * HALF],
                in_=relu[0, h][:].rearrange("p (r n) -> p r n", r=2),
                func=ACT.Square,
            )

        def square_scalar(a, r):
            nc.scalar.activation(out=result[a][:, r, :], in_=relu[a, r][:], func=ACT.Square)

        def square_vector(a, r):
            nc.vector.tensor_tensor(out=result[a][:, r, :], in0=relu[a, r][:], in1=relu[a, r][:], op=ALU.mult)

        out_rows = out_0.rearrange("(a p r) n -> a p r n", a=GROUPS, r=PACK)

        def store_result(a, r0, r1):
            nc.sync.dma_start(out=out_rows[a][:, r0:r1, :], in_=result[a][:, r0:r1, :])

        def round_result(copy, a, n0, n1):
            copy(
                out=result_bf16[a][:, PACK * n0 : PACK * n1].rearrange("p (c i r) -> p c r i", i=2, r=PACK),
                in_=result[a][:, :, n0:n1].rearrange("p r (c i) -> p c r i", i=2),
            )

        def quantize_result(a, n0, n1):
            nc.vector.quantize_mx(
                out=out_codes[a][:, n0:n1].bitcast(FP8X4),
                scales=out_scales[:, a, n0:n1],
                in_=result_bf16[a][:, PACK * n0 : PACK * n1],
            )

        def store_codes(a, n0, n1):
            words = out_1[a].rearrange("p n i -> p (n i)").bitcast(I32)
            nc.sync.dma_start(out=words[:, n0:n1], in_=out_codes[a][:, n0:n1])

        def store_scales(queue, q):
            queue.dma_start(
                out=out_2[:, 4 * q : 4 * q + 4, :].rearrange("a b n -> b a n").bitcast(I32),
                in_=out_scales[32 * q : 32 * q + 4, :, :].bitcast(I32),
            )

        on_vector = nc.vector.tensor_copy
        on_scalar = nc.scalar.copy

        upper_w(on_vector, 0, QUARTER)
        upper_w(on_scalar, QUARTER, HALF)
        for half in range(2):
            for pair in range(2):
                upper_x(0, pair, half)
        upper_w(on_scalar, HALF, M)
        for half in range(2):
            for pair in range(2):
                upper_x(1, pair, half)

        mask_w(0, QUARTER)
        mask_w(QUARTER, HALF)
        subtract_w(0, QUARTER)
        subtract_w(QUARTER, HALF)
        mask_x(0, 0, 0, 1)
        quantize_w(HI, 0, HALF)
        subtract_x(0, 0, 0)
        quantize_w(LO, 0, HALF)
        mask_x(0, 0, 1, 2)
        mask_x(0, 1, 0, 2)
        subtract_x(0, 0, 1)
        quantize_x(0, 0, HI)
        quantize_x(0, 0, LO)
        multiply_half(0)

        mask_w(HALF, M)
        quantize_x(0, 1, HI)
        subtract_w(HALF, M)
        quantize_w(HI, HALF, M)
        quantize_w(LO, HALF, M)
        multiply_half(1)
        multiply_hi(0, 1)
        relu_scalar(0, 0)
        relu_scalar(0, 1)
        square_half(0)
        square_half(1)
        store_result(0, 0, 2)

        subtract_x(0, 1, 0)
        mask_x(1, 0, 0, 2)
        subtract_x(0, 1, 1)
        quantize_x(1, 0, HI)
        subtract_x(1, 0, 0)
        quantize_x(0, 1, LO)
        multiply_lo(0, 1)
        multiply_hi(1, 0)
        relu_scalar(0, 2)
        relu_scalar(0, 3)
        square_scalar(0, 2)
        store_result(0, 2, 3)
        subtract_x(1, 0, 1)
        mask_x(1, 1, 0, 2)
        quantize_x(1, 0, LO)
        multiply_lo(1, 0)

        subtract_x(1, 1, 0)
        quantize_x(1, 1, HI)
        multiply_hi(1, 1)
        subtract_x(1, 1, 1)
        square_vector(0, 3)
        store_result(0, 3, 4)
        quantize_x(1, 1, LO)
        multiply_lo(1, 1)

        relu_scalar(1, 0)
        relu_scalar(1, 1)
        square_scalar(1, 0)
        store_result(1, 0, 1)
        square_scalar(1, 1)
        store_result(1, 1, 2)
        round_result(on_vector, 0, 0, HALF)
        relu_vector(1, 2)
        quantize_result(0, 0, HALF)
        square_vector(1, 2)
        store_result(1, 2, 3)
        relu_scalar(1, 3)
        square_scalar(1, 3)
        store_result(1, 3, 4)
        round_result(on_vector, 0, HALF, M)
        round_result(on_scalar, 1, 0, QUARTER)
        round_result(on_vector, 1, QUARTER, HALF)
        quantize_result(0, HALF, M)
        store_codes(0, 0, M)
        round_result(on_scalar, 1, HALF, HALF + QUARTER)
        round_result(on_vector, 1, HALF + QUARTER, M)
        quantize_result(1, 0, HALF)
        store_codes(1, 0, HALF)
        quantize_result(1, HALF, M)
        store_scales(nc.scalar, 0)
        store_scales(nc.sync, 1)
        store_scales(nc.scalar, 2)
        store_codes(1, HALF, M)
        store_scales(nc.sync, 3)
